import numpy as np
import ml_dtypes


def mxq(x, axis, fmt="e4m3"):
    dtype, down = {"e4m3": (ml_dtypes.float8_e4m3fn, 7), "e5m2": (ml_dtypes.float8_e5m2, 14)}[fmt]
    v = np.moveaxis(np.asarray(x, np.float32).astype(ml_dtypes.bfloat16).astype(np.float64), axis, -1)
    blocks = v.reshape(v.shape[:-1] + (-1, 32))
    amax = np.abs(blocks).max(-1, keepdims=True)
    byte = np.maximum(np.where(amax > 0, np.frexp(amax)[1] - 1 + 127, 0) - down, 1)
    scale = np.exp2(byte - 127.0)
    codes = (blocks / scale).astype(np.float32).astype(dtype).astype(np.float64)
    return np.moveaxis((codes * scale).reshape(v.shape), -1, axis)


WIDE = False


def mx_kscale(k):
    if not WIDE:
        return np.ones(k)
    levels = np.array([10, -10, 5, -5, 0])
    if k % 512:
        return np.exp2(np.random.permutation(np.resize(levels, k // 32))).repeat(32)
    a = np.empty((k // 512, 16))
    for p in range(k // 512):
        a[p, :8] = np.random.permutation(np.resize(levels, 8))
        for g in range(8):
            far = levels[np.abs(levels - a[p, g]) >= 10]
            a[p, g + 8] = far[np.random.randint(len(far))]
    return np.exp2(a.ravel()).repeat(32)


BF16 = ml_dtypes.bfloat16


def bf(x):
    return np.asarray(x, np.float32).astype(BF16)


def f64(x):
    return np.asarray(x).astype(np.float64)


N1, N2, D, T = 1024, 1024, 512, 4


def draw0():
    s, t = mx_kscale(D), mx_kscale(D)
    return {"e1": bf(np.random.standard_normal((N1, D)) * s),
            "e2": bf(np.random.standard_normal((N2, D)) / t),
            "w": bf(np.random.standard_normal((T, D, D)) / np.sqrt(D) / s[:, None] * t),
            "v": bf(np.random.standard_normal((T, D)) * 0.5 * t),
            "b": bf(0.3 + 0.1 * np.random.standard_normal(T)),
            "u": bf(np.random.uniform(0.5, 1.5, T))}


def core(e1, e2, w, v, b, u):
    scale = 1.0 / np.sqrt(e1.shape[1])
    t = mxq(f64(e1), 1, "e4m3") @ mxq(f64(w), 1, "e4m3")
    h = t + f64(v)[:, None, :]
    s = scale * (mxq(h, 2, "e4m3") @ mxq(f64(e2), 1, "e4m3").T)
    z = np.tanh(s + f64(b)[:, None, None])
    return np.sum(f64(u)[:, None, None] * z, axis=0)


def e4m3fn_bytes(y):
    return np.clip(np.asarray(y, np.float64), -448.0, 448.0).astype(np.float32).astype(ml_dtypes.float8_e4m3fn).view(np.uint8)


def e4m3fn_values(b):
    return np.asarray(b, np.uint8).view(ml_dtypes.float8_e4m3fn).astype(np.float64)


def setup_inputs():
    d = draw0()
    x0 = np.asarray(d['e2']).astype(np.float64)
    s = (np.max(np.abs(x0), axis=(0,), keepdims=True) / 448.0).astype(np.float32)
    out = {}
    for k, v in d.items():
        if k == 'e2':
            out['e2_bytes'] = e4m3fn_bytes(x0 / s.astype(np.float64))
            out['e2_scale'] = s
        else:
            out[k] = v
    return out


def reference(e1, e2_bytes, e2_scale, w, v, b, u):
    return core(e1, e4m3fn_values(e2_bytes) * e2_scale.astype(np.float64), w, v, b, u)

from contextlib import ExitStack

import concourse.mybir as mybir
from concourse.masks import make_identity

N1, N2, D, T = 1024, 1024, 512, 4
FLOPS = 2 * T * N1 * D * D + 2 * T * N1 * N2 * D

F32 = mybir.dt.float32
BF16 = mybir.dt.bfloat16
U32 = mybir.dt.uint32
U8 = mybir.dt.uint8
F8 = mybir.dt.float8_e4m3fn
FP8X4 = mybir.dt.float8_e4m3fn_x4
MULT = mybir.AluOpType.mult
ADD = mybir.AluOpType.add
TANH = mybir.ActivationFunctionType.Tanh
COPY = mybir.ActivationFunctionType.Copy

P = 128
PE_SUM = ((0, 1), (2, 1), (4, 1), (6, 1))
TS_ON_S = (5, 7)


def tile_pairwiseneuraltensorscorer_kernel(tc, e1, e2_bytes, e2_scale, w, v, b, u, out):
    nc = tc.nc
    with ExitStack() as ctx:
        keep = ctx.enter_context(tc.tile_pool(name="keep", bufs=1))
        work = ctx.enter_context(tc.tile_pool(name="work", bufs=2))
        psum_h = ctx.enter_context(tc.psum_pool(name="psum_h", bufs=2))
        psum_s = ctx.enter_context(tc.psum_pool(name="psum_s", bufs=4))
        psum_d = ctx.enter_context(tc.psum_pool(name="psum_d", bufs=2))
        ctx.enter_context(tc.manual_schedule())

        ident = keep.tile([P, P], F32, name="ident")
        warm = keep.tile([P, 1], F32, name="warm")
        scale_p = keep.tile([P, 4], F32, name="scale_p")
        scale_b = keep.tile([P, D], F32, name="scale_b", align_bytes=64)
        v4 = keep.tile([P, T, 4], BF16, name="v4")
        b_raw = keep.tile([P, T], BF16, name="b_raw")
        u_raw = keep.tile([P, T], BF16, name="u_raw")
        bu = keep.tile([P, 2, T], F32, name="bu")
        e2raw = [keep.tile([P, 4, D], U8, name="e2raw%d" % h, align_bytes=64) for h in range(2)]
        e1raw = [keep.tile([P, 4, D], BF16, name="e1raw%d" % h, align_bytes=64) for h in range(2)]
        wraw = [keep.tile([P, 4, D], BF16, name="wraw%d" % t, align_bytes=64) for t in range(T)]
        e2g = [keep.tile([P, 2048], BF16, name="e2g%d" % h, align_bytes=64) for h in range(2)]
        e1g = [keep.tile([P, 2048], BF16, name="e1g%d" % h, align_bytes=64) for h in range(2)]
        wg = [keep.tile([P, 2048], BF16, name="wg%d" % t, align_bytes=64) for t in range(T)]
        e2q = [keep.tile([P, 512], U32, name="e2q%d" % h, align_bytes=64) for h in range(2)]
        e2s = [keep.tile([P, 512], U8, name="e2s%d" % h, align_bytes=64) for h in range(2)]
        e1q = [keep.tile([P, 512], U32, name="e1q%d" % h, align_bytes=64) for h in range(2)]
        e1s = [keep.tile([P, 512], U8, name="e1s%d" % h, align_bytes=64) for h in range(2)]
        wq = [keep.tile([P, 512], U32, name="wq%d" % t, align_bytes=64) for t in range(T)]
        ws = [keep.tile([P, 512], U8, name="ws%d" % t, align_bytes=64) for t in range(T)]
        udiag = [keep.tile([P, P], F32, name="udiag%d" % t) for t in range(T)]

        nc.scalar.dma_start(out=scale_p[:], in_=e2_scale.rearrange("o (p t) -> p (o t)", t=4))
        nc.scalar.dma_start(out=v4[:], in_=v.rearrange("t (p s) -> p t s", s=4))
        nc.scalar.dma_start(out=b_raw[:], in_=b.partition_broadcast(P))
        nc.scalar.dma_start(out=u_raw[:], in_=u.partition_broadcast(P))

        def load_e2(h):
            nc.sync.dma_start(out=e2raw[h][:], in_=e2_bytes[512 * h : 512 * h + 512, :].rearrange("(n p) e -> p n e", p=P))

        def load_e1(h):
            nc.sync.dma_start(out=e1raw[h][:], in_=e1[512 * h : 512 * h + 512, :].rearrange("(p n) d -> p n d", n=4))

        def load_w(t):
            nc.sync.dma_start(out=wraw[t][:], in_=w[t].rearrange("(p j) e -> p j e", j=4))

        load_e2(0)
        load_e1(0)
        load_w(0)
        load_e2(1)
        load_w(1)
        load_w(2)
        load_e1(1)
        load_w(3)

        make_identity(nc, ident[:])
        nc.gpsimd.memset(warm[:], 0.0)
        nc.scalar.activation(out=warm[:], in_=warm[:], func=TANH)

        def transpose_words(dst, rows, n):
            words = rows.bitcast(F32)
            for half in range(2):
                nc.tensor.transpose(dst[:, n, half, :], words[:, half : 256 : 2], ident[:])

        def empty_words(grouped, pair, bank):
            nc.scalar.copy(
                out=grouped[:].bitcast(F32)[:, 512 * pair : 512 * pair + 512].rearrange("p (n r q) -> p n r q", n=2, q=2),
                in_=bank[:].rearrange("p n q r -> p n r q"),
            )

        def quantize(codes, scales, grouped):
            nc.vector.quantize_mx(out=codes.bitcast(FP8X4), scales=scales, in_=grouped)

        e2rows = {}

        def widen(h, n):
            rows = work.tile([P, D], BF16, name="e2rows", bufs=4, align_bytes=64)
            nc.vector.tensor_tensor(out=rows[:], in0=e2raw[h][:, n, :].bitcast(F8), in1=scale_b[:], op=MULT)
            e2rows[(h, n)] = rows

        tbank = {}

        def e2_turn(h, pair):
            bank = psum_h.tile([P, 2, 2, P], F32, name="bank_h")
            for n in range(2):
                transpose_words(bank, e2rows[(h, 2 * pair + n)][:], n)
            tbank[("e2", h, pair)] = bank

        def e1_turn(h, pair):
            bank = psum_h.tile([P, 2, 2, P], F32, name="bank_h")
            for n in range(2):
                transpose_words(bank, e1raw[h][:, 2 * pair + n, :], n)
            tbank[("e1", h, pair)] = bank

        def e2_empty(h, pair):
            empty_words(e2g[h], pair, tbank[("e2", h, pair)])

        def e1_empty(h, pair):
            empty_words(e1g[h], pair, tbank[("e1", h, pair)])

        def w_piece(t, s, engine_copy):
            engine_copy(
                out=wg[t][:, 512 * s : 512 * s + 512].rearrange("p (m j) -> p m j", j=4),
                in_=wraw[t][:].rearrange("p j (m s) -> p s m j", s=4)[:, s],
            )

        slots = [(i, t) for t in range(T) for i in range(4)] + [(i + k, t) for i in (4, 6) for t in range(T) for k in range(2)]
        S = len(slots)
        hbank, hg, hq, hs, sbank, z, acc, dbank = {}, {}, {}, {}, {}, {}, {}, {}

        def stage1(x):
            i, t = slots[x]
            bank = psum_h.tile([P, 4, P], F32, name="bank_h")
            cols = slice(128 * (i % 4), 128 * (i % 4) + 128)
            for s in range(4):
                nc.tensor.matmul_mx(
                    out=bank[:, s, :],
                    lhsT=wq[t][:, 128 * s : 128 * s + 128].bitcast(FP8X4),
                    lhsT_scale=ws[t][:, 128 * s : 128 * s + 128],
                    rhs=e1q[i // 4][:, cols].bitcast(FP8X4),
                    rhs_scale=e1s[i // 4][:, cols],
                    start=True,
                    stop=True,
                )
            hbank[x] = bank

        def evac(x):
            i, t = slots[x]
            if x % 2 == 0:
                g = work.tile([P, 2, P, 4], BF16, name="hg", bufs=3, align_bytes=64)
                hg[x // 2] = g
            nc.vector.tensor_tensor(
                out=hg[x // 2][:, x % 2],
                in0=hbank[x][:].rearrange("p s r -> p r s"),
                in1=v4[:, t : t + 1, :].to_broadcast([P, P, 4]),
                op=ADD,
            )

        def quant(pair):
            q = work.tile([P, 2 * P], U32, name="hq", bufs=3, align_bytes=64)
            sc = work.tile([P, 2 * P], U8, name="hs", bufs=3, align_bytes=64)
            quantize(q[:], sc[:], hg[pair][:].rearrange("p x r s -> p (x r s)"))
            hq[pair], hs[pair] = q, sc

        def stage2(x, jh):
            bank = psum_s.tile([P, 512], F32, name="bank_s")
            nc.tensor.matmul_mx(
                out=bank[:],
                lhsT=hq[x // 2][:, P * (x % 2) : P * (x % 2) + P].bitcast(FP8X4),
                lhsT_scale=hs[x // 2][:, P * (x % 2) : P * (x % 2) + P],
                rhs=e2q[jh][:].bitcast(FP8X4),
                rhs_scale=e2s[jh][:],
                start=True,
                stop=True,
            )
            sbank[(x, jh)] = bank

        def tanh(x, jh):
            i, t = slots[x]
            if jh == 0:
                on_pe = (i, 0) in PE_SUM or (i, 1) in PE_SUM
                if on_pe:
                    zd = work.tile([P, N2], F32, name="zd", bufs=8)
                    z[x] = zd
                else:
                    zt = work.tile([P, N2], F32, name="z", bufs=6)
                    z[x] = zt
            nc.scalar.activation(
                out=z[x][:, 512 * jh : 512 * jh + 512], in_=sbank[(x, jh)][:], func=TANH, bias=bu[:, 0, t : t + 1], scale=1.0 / D**0.5
            )

        def get_acc(i):
            if i not in acc:
                a = work.tile([P, N2], F32, name="acc", bufs=6)
                acc[i] = a
            return acc[i]

        def store(i, cols):
            rows = out[512 * (i // 4) : 512 * (i // 4) + 512, :].rearrange("(p n) j -> p n j", n=4)
            nc.sync.dma_start(out=rows[:, i % 4, cols], in_=acc[i][:, cols])

        def vcols(i):
            return [slice(512 * jh, 512 * jh + 512) for jh in range(2) if (i, jh) not in PE_SUM]

        def sum_v(x):
            i, t = slots[x]
            ucol = bu[:, 1, t : t + 1]
            cols = vcols(i)
            if len(cols) == 2 and x < S - 1:
                cols = [slice(0, N2)]
            if t == 0 and i in TS_ON_S:
                return
            for c in cols:
                a = get_acc(i)
                if t == 0:
                    nc.vector.tensor_scalar(out=a[:, c], in0=z[x][:, c], scalar1=ucol, scalar2=None, op0=MULT)
                else:
                    nc.vector.scalar_tensor_tensor(out=a[:, c], in0=z[x][:, c], scalar=ucol, in1=a[:, c], op0=MULT, op1=ADD)
                if t == T - 1:
                    store(i, c)

        def sum_s(x):
            i, t = slots[x]
            if t == 0 and i in TS_ON_S:
                cols = vcols(i)
                a = get_acc(i)
                c = slice(0, 512 * len(cols))
                nc.scalar.activation(out=a[:, c], in_=z[x][:, c], func=COPY, scale=bu[:, 1, 0:1])

        def sum_pe(item):
            x, jh = item
            i, t = slots[x]
            if t == 0:
                bank = psum_d.tile([P, 512], F32, name="bank_d")
                dbank[(i, jh)] = bank
            nc.tensor.matmul(
                out=dbank[(i, jh)][:], lhsT=udiag[t][:], rhs=z[x][:, 512 * jh : 512 * jh + 512], start=(t == 0), stop=(t == T - 1)
            )

        def empty_pe(i, jh):
            a = get_acc(i)
            c = slice(512 * jh, 512 * jh + 512)
            nc.scalar.copy(out=a[:, c], in_=dbank[(i, jh)][:])
            store(i, c)

        bank = psum_h.tile([P, 4, P], F32, name="bank_h")
        for q in range(4):
            nc.tensor.transpose(bank[:, q, :], scale_p[:, q : q + 1].to_broadcast([P, P]), ident[:])
        nc.scalar.copy(out=scale_b[:].rearrange("p (n q) -> p n q", q=4), in_=bank[:].rearrange("p q n -> p n q"))
        nc.gpsimd.tensor_copy(out=bu[:, 0, :], in_=b_raw[:])
        nc.gpsimd.tensor_copy(out=bu[:, 1, :], in_=u_raw[:])
        for t in range(T):
            nc.gpsimd.tensor_scalar(out=udiag[t][:], in0=ident[:], scalar1=bu[:, 1, t : t + 1], scalar2=None, op0=MULT)
        e1_turn(0, 0)
        e1_empty(0, 0)
        e1_turn(0, 1)
        e1_empty(0, 1)
        widen(0, 0)
        widen(0, 1)
        e2_turn(0, 0)
        widen(0, 2)
        widen(0, 3)
        e2_turn(0, 1)
        quantize(e1q[0][:], e1s[0][:], e1g[0][:])
        widen(1, 0)
        widen(1, 1)
        w_piece(0, 0, nc.scalar.copy)
        w_piece(0, 1, nc.scalar.copy)
        w_piece(0, 2, nc.scalar.copy)
        w_piece(0, 3, nc.scalar.copy)
        e2_empty(0, 0)
        e2_empty(0, 1)
        quantize(wq[0][:], ws[0][:], wg[0][:])
        widen(1, 2)
        e2_turn(1, 0)
        stage1(0)
        widen(1, 3)
        w_piece(1, 0, nc.scalar.copy)
        e2_empty(1, 0)
        quantize(e2q[0][:], e2s[0][:], e2g[0][:])
        stage1(1)
        e2_turn(1, 1)
        evac(0)
        w_piece(1, 1, nc.scalar.copy)
        w_piece(1, 2, nc.scalar.copy)
        e2_empty(1, 1)
        evac(1)
        w_piece(1, 3, nc.scalar.copy)
        quantize(e2q[1][:], e2s[1][:], e2g[1][:])
        quant(0)
        stage1(2)
        stage2(0, 0)
        stage2(0, 1)
        stage1(3)
        stage2(1, 0)
        stage2(1, 1)
        evac(2)
        quantize(wq[1][:], ws[1][:], wg[1][:])
        evac(3)
        w_piece(2, 0, nc.scalar.copy)
        w_piece(2, 1, nc.scalar.copy)
        w_piece(2, 2, nc.scalar.copy)
        quant(1)
        stage1(4)
        stage1(5)

        queue = [(x, jh) for x in range(S) for jh in range(2) if (slots[x][0], jh) in PE_SUM]
        done = []
        wtodo = [(t, s) for t in range(2, T) for s in range(4)][3:]
        pairs = S // 2
        for p in range(pairs + 3):
            a, b = 2 * p + 4, 2 * p + 5
            if p + 1 < pairs:
                stage2(2 * p + 2, 0)
                stage2(2 * p + 2, 1)
            if p + 3 < pairs:
                stage1(a + 2)
            if p == 3:
                e1_turn(1, 0)
            if queue and queue[0][0] + 2 <= 2 * p:
                item = queue.pop(0)
                sum_pe(item)
                if slots[item[0]][1] == T - 1:
                    done.append((p, slots[item[0]][0], item[1]))
            if p + 1 < pairs:
                stage2(2 * p + 3, 0)
                stage2(2 * p + 3, 1)
            if p + 3 < pairs:
                stage1(b + 2)
            if p == 3:
                e1_turn(1, 1)
            for x in (2 * p, 2 * p + 1):
                if x < S:
                    tanh(x, 0)
                    tanh(x, 1)
                    sum_s(x)
                    if wtodo and p >= 0:
                        w_piece(*wtodo.pop(0), nc.scalar.copy)
            if p == 3:
                e1_empty(1, 0)
                e1_empty(1, 1)
            if done and done[0][0] < p:
                empty_pe(*done.pop(0)[1:])
            if p + 2 < pairs:
                evac(a)
            if 0 < p <= pairs:
                sum_v(2 * p - 2)
            if p + 2 < pairs:
                evac(b)
            if 0 < p <= pairs:
                sum_v(2 * p - 1)
            if p + 2 < pairs:
                quant(p + 2)
            if p in (99, 0, 2):
                t = 1 + (99, 0, 2).index(p)
                quantize(wq[t][:], ws[t][:], wg[t][:])
            if p == 4:
                quantize(e1q[1][:], e1s[1][:], e1g[1][:])
